import numpy as np, ml_dtypes
CORES = [3,19,35,51,67,83,147,179]
N = 8
import mx_ref
NC = 128
BF = ml_dtypes.bfloat16
def cut(t, i, w=512):
    return t[:, w * i:w * i + w]
def term(a, B):
    return np.stack([mx_ref.matmul(mx_ref.quantize(cut(a, i)), B) for i in range(4)], axis=2).reshape(128, -1)
def setup_inputs(rng):
    def f(*shape):
        return mx_ref.flush((rng.standard_normal(shape, dtype=np.float32) * np.exp2(rng.integers(-2, 3, shape[:-1] + (1,)))).astype(BF))
    return {"a": f(N, 128, 4 * 512), "b": f(N, 128, N * 4 * NC)}
def setup_inputs_blocks(rng):
    d = setup_inputs(rng)
    for k in ("a", "b"): d[k] = mx_ref.spread(d[k], rng, 2)
    return d
def setup_inputs_wide(rng):
    d = setup_inputs(rng)
    for k in ("a", "b"): d[k] = mx_ref.flush((d[k].astype(np.float32) * np.exp2(rng.integers(-4, 5, (N, 1, 1))).astype(np.float32)).astype(BF))
    return d
def setup_inputs_lossless(rng):
    a = np.zeros((N, 128, 4 * 128, 4), np.float32)
    for r in range(N):
        k = rng.integers(0, 512, size=4 * 128)
        a[r, k // 4, np.arange(4 * 128), k % 4] = 1.0
    size = np.repeat(2.0 ** rng.integers(-4, 5, size=(1, 1, (N * 4 * NC) // 4)), 4, axis=2)
    b = rng.integers(-1, 2, size=(N, 128, N * 4 * NC)) * size
    return {"a": a.reshape(N, 128, 4 * 512).astype(BF), "b": b.astype(np.float32).astype(BF)}
def reference(a, b):
    y = np.zeros((N, 128, 4 * NC), np.float32)
    for c in range(N):
        y[c] = mx_ref.total([term(a[r], mx_ref.quantize(cut(b[r], c, 4 * NC))) for r in range(N)])
    return {"y": y}

@@ -1,0 +1,232 @@
+from concourse.bass import DstId, RemoteDMATransfer
+from concourse.mybir import dt, AluOpType, ActivationFunctionType
+
+W = 128
+E = 4 * W
+BANK = 512
+NR = 8
+MAXG = 5
+
+SCRATCH = {
+    "at": ("sbuf", [128, 4 * E], "bfloat16"),
+    "bt": ("sbuf", [128, NR * E], "bfloat16"),
+    "aq": ("sbuf", [128, 4 * W], "float8_e4m3fn_x4"),
+    "ap": ("sbuf", [128, 4 * W], "uint8"),
+    "bq": ("sbuf", [128, NR * W], "float8_e4m3fn_x4"),
+    "bp": ("sbuf", [128, NR * W], "uint8"),
+    "one": ("sbuf", [128, W], "bfloat16"),
+    "st": ("sbuf", [128, 4 * E], "bfloat16"),
+    "sq": ("sbuf", [128, 4 * W], "float8_e4m3fn_x4"),
+    "sp": ("sbuf", [128, 4 * W], "uint8"),
+    "ht": ("sbuf", [128, NR * E], "bfloat16"),
+    "hq": ("sbuf", [128, NR * W], "float8_e4m3fn_x4"),
+    "hp": ("sbuf", [128, NR * W], "uint8"),
+    "lq": ("sbuf", [128, NR * W], "float8_e4m3fn_x4"),
+    "lp": ("sbuf", [128, NR * W], "uint8"),
+    "mq": ("sbuf", [128, 2 * W], "float8_e4m3fn_x4"),
+    "mp": ("sbuf", [128, 2 * W], "uint8"),
+    "yt": ("sbuf", [128, E], "float32"),
+    "ps": ("psum", [128, 8 * BANK], "float32"),
+}
+SEMAPHORES = (["lda0", "lda1", "fill", "pick", "qs", "qa0", "qa1", "marr", "sent", "yev", "stored"]
+              + ["ldb%d" % k for k in range(5)] + ["qb%d" % k for k in range(5)]
+              + ["mm%d_%d" % (k, i) for k in range(MAXG) for i in range(4)]
+              + ["ev%d" % k for k in range(MAXG)] + ["qh%d" % k for k in range(MAXG)]
+              + ["arr%d" % k for k in range(NR)] + ["fin%d" % i for i in range(4)])
+
+
+def pairs_of(T, topo):
+    hosts = {}
+    for r, c in enumerate(T.cores):
+        hosts.setdefault(topo.host(c), []).append(r)
+    far, big = sorted(hosts.values(), key=len)
+    return [big[k:k + 2] for k in range(0, len(big), 2)], far
+
+
+def plan_of(T, topo, r):
+    near, far = pairs_of(T, topo)
+    if r in far:
+        k = far.index(r)
+        y = far[1 - k]
+        q, m = near[2], near[1 - k]
+        return y, [near[k], q, far, m], [near[k], q, [y], m], [q, [y], m]
+    p = [r in q for q in near].index(True)
+    k = near[p].index(r)
+    y = near[p][1 - k]
+    q1, q2, m = near[(p + 1) % 3], near[(p + 2) % 3], far[k]
+    f = far[1 - k]
+    return y, [[f], q1, q2, near[p], [m]], [[f], q1, q2, [y], [m]], [q1, q2, [y, m]]
+
+
+def share(mask, k):
+    bits = [1 << e for e in range(16) if mask >> e & 1]
+    n = 1
+    while 2 * n * k <= len(bits):
+        n *= 2
+    return [sum(bits[n * j:n * j + n]) for j in range(k)]
+
+
+def calls_of(T, topo, r):
+    c = T.cores[r]
+    y, _, groups, sends = plan_of(T, topo, r)
+    flat = [t for q in groups for t in q]
+    of = [gi for gi, q in enumerate(groups) for t in q]
+    d = T.cores[y]
+    out = [(part, 0, [(d, 0, "m", 0, W * len(groups[0]), "marr", topo.mask(c, d))]) for part in "qp"]
+    for tiles in sends:
+        ms = share(topo.mask(c, T.cores[tiles[0]]), len(tiles))
+        for part in "qp":
+            out.append((part, max(of[flat.index(t)] for t in tiles),
+                        [(T.cores[t], W * flat.index(t), "l", r * W, W, "arr%d" % r, e) for t, e in zip(tiles, ms)]))
+    return out
+
+
+def issue(g, T, topo, core, call):
+    part, _, dests = call
+    items = []
+    for (d, at, dst, to, n, sem, mask) in dests:
+        o = T[dst + part][:, to:to + n]
+        i = T["h" + part][:, at:at + n]
+        if part == "q":
+            o, i = o.bitcast(dt.uint8), i.bitcast(dt.uint8)
+        rid, pid = topo.addr(d, core)
+        items.append((o, i, T.sem[sem], rid, pid, mask))
+    if len(items) == 1:
+        o, i, sem, rid, pid, mask = items[0]
+        g.remote_dma(o, i, sem, T.sem.sent, pid, rid, mask)
+    else:
+        g.remote_dma_fused([RemoteDMATransfer(dst_ids=[DstId(rid=rid, pnc=pid)], dma_engine_mask=mask,
+                                              remote_sem=sem, src=i, dst=o)
+                            for o, i, sem, rid, pid, mask in items], local_sem=T.sem.sent)
+    return sum(bin(x[5]).count("1") for x in items)
+
+
+def arrivals(T, topo, core):
+    got = {}
+    for r in range(NR):
+        for k, (_, _, dests) in enumerate(calls_of(T, topo, r)):
+            for x in dests:
+                if x[0] == core:
+                    got[x[5]] = (k, got.get(x[5], (0, 0))[1] + bin(x[6]).count("1"))
+    return got
+
+
+def rank_program(g, core, T, topo):
+    rank = T.rank_of(core)
+    if rank is None:
+        return
+    S = T.sem
+    V, X, A = g.vector, g.tensor, g.scalar
+    got = arrivals(T, topo, core)
+    _, loads, groups, _ = plan_of(T, topo, rank)
+    ng = len(groups)
+    where = {t: k for k, tiles in enumerate(loads) for t in tiles}
+
+    q = [g.sync, g.scalar]
+    for k in range(2):
+        w = slice(2 * E * k, 2 * E * (k + 1))
+        q[k].dma_start(T.at[:, w], T.a[:, w]).then_inc(S["lda%d" % k], 16)
+    for k, tiles in enumerate(loads):
+        w = slice(E * tiles[0], E * (tiles[-1] + 1))
+        q[k % 2].dma_start(T.bt[:, w], T.b[:, w]).then_inc(S["ldb%d" % k], 16)
+
+    V.memset(T.one[:], 1.0).then_inc(S.fill, 1)
+    V.memset(T.st[:], 0.0).then_inc(S.fill, 1)
+    g.wait_ge(S.fill, 2)
+    for i in range(4):
+        g.affine_select(T.st[:, E * i + i:E * (i + 1):4], T.one[:], [[-1, W]], AluOpType.is_equal, 0.0, 0, 1).then_inc(S.pick, 1)
+    V.wait_ge(S.pick, 4)
+    V.quantize_mx(T.sq[:], T.sp[:], T.st[:]).then_inc(S.qs, 1)
+
+    for k in range(2):
+        V.wait_ge(S["lda%d" % k], 16)
+        w = slice(2 * W * k, 2 * W * (k + 1))
+        V.quantize_mx(T.aq[:, w], T.ap[:, w], T.at[:, 2 * E * k:2 * E * (k + 1)]).then_inc(S["qa%d" % k], 1)
+
+    def quantise_b(k):
+        tiles = loads[k]
+        w = slice(W * tiles[0], W * (tiles[-1] + 1))
+        V.wait_ge(S["ldb%d" % k], 16)
+        V.quantize_mx(T.bq[:, w], T.bp[:, w], T.bt[:, E * tiles[0]:E * (tiles[-1] + 1)]).then_inc(S["qb%d" % k], 1)
+
+    def stat(i):
+        return T.aq[:, W * i:W * (i + 1)], T.ap[:, W * i:W * (i + 1)]
+
+    def pick(i):
+        return T.sq[:, W * i:W * (i + 1)], T.sp[:, W * i:W * (i + 1)]
+
+    def bank(s, i, n):
+        k = BANK * (4 * (s % 2) + i)
+        return T.ps[:, k:k + n]
+
+    quantise_b(0)
+    off = 0
+    for gi, tiles in enumerate(groups):
+        n = len(tiles) * W
+        merge = gi == ng - 1
+        w = slice(W * tiles[0], W * tiles[0] + n)
+        X.wait_ge(S["qb%d" % where[tiles[0]]], 1)
+        if gi >= 2:
+            X.wait_ge(S["ev%d" % (gi - 2)], 4)
+        for i in range(4):
+            if gi == 0 and i % 2 == 0:
+                X.wait_ge(S["qa%d" % (i // 2)], 1)
+            m = X.matmul_mx(bank(gi, i, n), *stat(i), T.bq[:, w], T.bp[:, w], True, not merge)
+            if not merge:
+                m.then_inc(S["mm%d_%d" % (gi, i)], 1)
+        if merge:
+            X.wait_ge(S["qb%d" % where[rank]], 1)
+            X.wait_ge(S["ev%d" % (gi - 1)], 4)
+            o = slice(W * rank, W * (rank + 1))
+            for i in range(4):
+                X.matmul_mx(bank(gi + 1, i, W), *stat(i), T.bq[:, o], T.bp[:, o], True, False)
+            X.wait_ge(S.qs, 1)
+            X.wait_ge(S.marr, got["marr"][1])
+            for i in range(4):
+                X.matmul_mx(bank(gi, i, n), *pick(i), T.mq[:, 0:n], T.mp[:, 0:n], False, True).then_inc(S["mm%d_%d" % (gi, i)], 1)
+        if gi > 0 and gi + 1 < len(loads):
+            quantise_b(gi + 1)
+        onv = (1, 3) if gi == 0 or merge else (3,)
+        for i in range(4):
+            out = T.ht[:, 4 * off + i:4 * (off + n):4]
+            if i not in onv:
+                A.wait_ge(S["mm%d_%d" % (gi, i)], 1)
+                A.activation(out, bank(gi, i, n), ActivationFunctionType.Copy).then_inc(S["ev%d" % gi], 1)
+            else:
+                V.wait_ge(S["mm%d_%d" % (gi, i)], 1)
+                V.tensor_copy(out, bank(gi, i, n)).then_inc(S["ev%d" % gi], 1)
+        V.wait_ge(S["ev%d" % gi], 4)
+        V.quantize_mx(T.hq[:, off:off + n], T.hp[:, off:off + n], T.ht[:, 4 * off:4 * (off + n)]).then_inc(S["qh%d" % gi], 1)
+        if gi == 0:
+            quantise_b(1)
+        off += n
+
+    total, ready = 0, -1
+    for call in calls_of(T, topo, rank):
+        while ready < call[1]:
+            ready += 1
+            g.wait_ge(S["qh%d" % ready], 1)
+        total += issue(g, T, topo, core, call)
+
+    order = sorted((k, name) for name, (k, _) in got.items() if name != "marr")
+    for j, (_, name) in enumerate(order):
+        r = int(name[3:])
+        X.wait_ge(S[name], got[name][1])
+        w = slice(W * r, W * (r + 1))
+        end = j == len(order) - 1
+        for i in range(4):
+            m = X.matmul_mx(bank(ng, i, W), *pick(i), T.lq[:, w], T.lp[:, w], False, end)
+            if end:
+                m.then_inc(S["fin%d" % i], 1)
+    for i in range(4):
+        out = T.yt[:, i:E:4]
+        if i % 2 == 0:
+            A.wait_ge(S["fin%d" % i], 1)
+            A.activation(out, bank(ng, i, W), ActivationFunctionType.Copy).then_inc(S.yev, 1)
+        else:
+            V.wait_ge(S["fin%d" % i], 1)
+            V.tensor_copy(out, bank(ng, i, W)).then_inc(S.yev, 1)
+    g.sync.wait_ge(S.yev, 4)
+    g.sync.dma_start(T.y[:], T.yt[:]).then_inc(S.stored, 16)
+    g.sync.wait_ge(S.stored, 16)
+    g.wait_ge(S.sent, total)

@@ -6,6 +6,7 @@ E = 4 * W
 BANK = 512
 NR = 8
 MAXG = 5
+CUTS = [0, 3, 4]
 
 SCRATCH = {
     "at": ("sbuf", [128, 4 * E], "bfloat16"),
@@ -15,12 +16,14 @@ SCRATCH = {
     "bq": ("sbuf", [128, NR * W], "float8_e4m3fn_x4"),
     "bp": ("sbuf", [128, NR * W], "uint8"),
     "one": ("sbuf", [128, W], "bfloat16"),
-    "st": ("sbuf", [128, 4 * E], "bfloat16"),
+    "st": ("sbuf", [128, E], "bfloat16"),
     "sq": ("sbuf", [128, 4 * W], "float8_e4m3fn_x4"),
     "sp": ("sbuf", [128, 4 * W], "uint8"),
     "ht": ("sbuf", [128, NR * E], "bfloat16"),
     "hq": ("sbuf", [128, NR * W], "float8_e4m3fn_x4"),
     "hp": ("sbuf", [128, NR * W], "uint8"),
+    "rq": ("sbuf", [128, 2 * W], "float8_e4m3fn_x4"),
+    "rp": ("sbuf", [128, 2 * W], "uint8"),
     "lq": ("sbuf", [128, NR * W], "float8_e4m3fn_x4"),
     "lp": ("sbuf", [128, NR * W], "uint8"),
     "mq": ("sbuf", [128, 2 * W], "float8_e4m3fn_x4"),
@@ -28,7 +31,7 @@ SCRATCH = {
     "yt": ("sbuf", [128, E], "float32"),
     "ps": ("psum", [128, 8 * BANK], "float32"),
 }
-SEMAPHORES = (["lda0", "lda1", "fill", "pick", "qs", "qa0", "qa1", "marr", "sent", "yev", "stored"]
+SEMAPHORES = (["lda0", "lda1", "fill", "pick", "qs", "qa0", "qa1", "sarr", "marr", "rqarr", "rparr", "sent", "yev", "stored"]
               + ["ldb%d" % k for k in range(5)] + ["qb%d" % k for k in range(5)]
               + ["mm%d_%d" % (k, i) for k in range(MAXG) for i in range(4)]
               + ["ev%d" % k for k in range(MAXG)] + ["qh%d" % k for k in range(MAXG)]
@@ -49,13 +52,20 @@ def plan_of(T, topo, r):
         k = far.index(r)
         y = far[1 - k]
         q, m = near[2], near[1 - k]
-        return y, [near[k], q, far, m], [near[k], q, [y], m], [q, [y], m]
+        return y, k, [near[k], q, far, m], [near[k], q, [y], m], [(q, False), ([y], False), (m, False)]
     p = [r in q for q in near].index(True)
     k = near[p].index(r)
     y = near[p][1 - k]
     q1, q2, m = near[(p + 1) % 3], near[(p + 2) % 3], far[k]
     f = far[1 - k]
-    return y, [[f], q1, q2, near[p], [m]], [[f], q1, q2, [y], [m]], [q1, q2, [y, m]]
+    return y, k, [[f], q1, q2, near[p], [m]], [[f], q1, q2, [y], [m]], [(q1, True), (q2, False), ([y, m], False)]
+
+
+def helper_of(T, topo, r):
+    c = T.cores[r]
+    for d in range(256):
+        if topo.host(d) == topo.host(c) and topo.chip(d) == topo.chip(c) and topo.die(d) != topo.die(c):
+            return d
 
 
 def share(mask, k):
@@ -67,26 +77,40 @@ def share(mask, k):
 
 
 def calls_of(T, topo, r):
-    c = T.cores[r]
-    y, _, groups, sends = plan_of(T, topo, r)
+    c, h = T.cores[r], helper_of(T, topo, r)
+    y, k, _, groups, sends = plan_of(T, topo, r)
     flat = [t for q in groups for t in q]
     of = [gi for gi, q in enumerate(groups) for t in q]
     d = T.cores[y]
-    out = [(part, 0, [(d, 0, "m", 0, W * len(groups[0]), "marr", topo.mask(c, d))]) for part in "qp"]
-    for tiles in sends:
-        ms = share(topo.mask(c, T.cores[tiles[0]]), len(tiles))
-        for part in "qp":
-            out.append((part, max(of[flat.index(t)] for t in tiles),
-                        [(T.cores[t], W * flat.index(t), "l", r * W, W, "arr%d" % r, e) for t, e in zip(tiles, ms)]))
+    e = topo.mask(c, d)
+    near = topo.mask(c, h) & ~e
+    out = []
+    for part in "qp":
+        out.append((c, part, ["qs"], 0, [(d, "s", W * k, "s", W * k, W, "sarr", e)]))
+        out.append((h, part, ["qs"], 0, [(x, "s", W * (2 + k), "s", W * (2 + k), W, "sarr", m)
+                                         for x, m in zip((c, d), share(topo.mask(h, d), 2))]))
+    out += [(c, part, ["qh0"], 0, [(d, "h", 0, "m", 0, W * len(groups[0]), "marr", e)]) for part in "qp"]
+    for place, (tiles, relay) in enumerate(sends):
+        at = W * flat.index(tiles[0])
+        waits = ["qh%d" % gi for gi in sorted({of[flat.index(t)] for t in tiles})]
+        if relay:
+            out += [(c, part, waits, 0, [(h, "h", at, "r", 0, W * len(tiles), "r%sarr" % part, near)]) for part in "qp"]
+            ms = share(topo.mask(h, T.cores[tiles[0]]), len(tiles))
+            out += [(h, part, ["r%sarr" % part], 1, [(T.cores[t], "r", W * j, "l", r * W, W, "arr%d" % r, x)
+                                                     for j, (t, x) in enumerate(zip(tiles, ms))]) for part in "qp"]
+        else:
+            ms = share(topo.mask(c, T.cores[tiles[0]]), len(tiles))
+            out += [(c, part, waits, place, [(T.cores[t], "h", W * flat.index(t), "l", r * W, W, "arr%d" % r, x)
+                                             for t, x in zip(tiles, ms)]) for part in "qp"]
     return out
 
 
 def issue(g, T, topo, core, call):
-    part, _, dests = call
+    part = call[1]
     items = []
-    for (d, at, dst, to, n, sem, mask) in dests:
+    for (d, src, at, dst, to, n, sem, mask) in call[4]:
         o = T[dst + part][:, to:to + n]
-        i = T["h" + part][:, at:at + n]
+        i = T[src + part][:, at:at + n]
         if part == "q":
             o, i = o.bitcast(dt.uint8), i.bitcast(dt.uint8)
         rid, pid = topo.addr(d, core)
@@ -101,52 +125,73 @@ def issue(g, T, topo, core, call):
     return sum(bin(x[5]).count("1") for x in items)
 
 
+def issue_all(g, T, topo, core, got):
+    total, seen = 0, []
+    for r in range(NR):
+        for call in calls_of(T, topo, r):
+            if call[0] == core:
+                for name in call[2]:
+                    if name not in seen:
+                        seen.append(name)
+                        g.wait_ge(T.sem[name], got[name][1] if name in got else 1)
+                total += issue(g, T, topo, core, call)
+    g.wait_ge(T.sem.sent, total)
+
+
 def arrivals(T, topo, core):
     got = {}
     for r in range(NR):
-        for k, (_, _, dests) in enumerate(calls_of(T, topo, r)):
-            for x in dests:
+        for _, _, _, place, items in calls_of(T, topo, r):
+            for x in items:
                 if x[0] == core:
-                    got[x[5]] = (k, got.get(x[5], (0, 0))[1] + bin(x[6]).count("1"))
+                    got[x[6]] = (place, got.get(x[6], (0, 0))[1] + bin(x[7]).count("1"))
     return got
+
+
+def make_pick(g, T, i):
+    S = T.sem
+    g.vector.memset(T.one[:], 1.0).then_inc(S.fill, 1)
+    g.vector.memset(T.st[:], 0.0).then_inc(S.fill, 1)
+    g.wait_ge(S.fill, 2)
+    g.affine_select(T.st[:, i:E:4], T.one[:], [[-1, W]], AluOpType.is_equal, 0.0, 0, 1).then_inc(S.pick, 1)
+    g.vector.wait_ge(S.pick, 1)
+    w = slice(W * i, W * (i + 1))
+    g.vector.quantize_mx(T.sq[:, w], T.sp[:, w], T.st[:]).then_inc(S.qs, 1)
 
 
 def rank_program(g, core, T, topo):
     rank = T.rank_of(core)
+    got = arrivals(T, topo, core)
     if rank is None:
+        helpers = [helper_of(T, topo, k) for k in range(NR)]
+        if core in helpers:
+            make_pick(g, T, 2 + plan_of(T, topo, helpers.index(core))[1])
+            issue_all(g, T, topo, core, got)
         return
     S = T.sem
     V, X, A = g.vector, g.tensor, g.scalar
-    got = arrivals(T, topo, core)
-    _, loads, groups, _ = plan_of(T, topo, rank)
+    _, me, loads, groups, _ = plan_of(T, topo, rank)
     ng = len(groups)
     where = {t: k for k, tiles in enumerate(loads) for t in tiles}
 
-    q = [g.sync, g.scalar]
     for k in range(2):
-        w = slice(2 * E * k, 2 * E * (k + 1))
-        q[k].dma_start(T.at[:, w], T.a[:, w]).then_inc(S["lda%d" % k], 16)
+        w = slice(E * CUTS[k], E * CUTS[k + 1])
+        g.sync.dma_start(T.at[:, w], T.a[:, w]).then_inc(S["lda%d" % k], 16)
     for k, tiles in enumerate(loads):
         w = slice(E * tiles[0], E * (tiles[-1] + 1))
-        q[k % 2].dma_start(T.bt[:, w], T.b[:, w]).then_inc(S["ldb%d" % k], 16)
+        (g.sync if k else g.scalar).dma_start(T.bt[:, w], T.b[:, w]).then_inc(S["ldb%d" % k], 16)
 
-    V.memset(T.one[:], 1.0).then_inc(S.fill, 1)
-    V.memset(T.st[:], 0.0).then_inc(S.fill, 1)
-    g.wait_ge(S.fill, 2)
-    for i in range(4):
-        g.affine_select(T.st[:, E * i + i:E * (i + 1):4], T.one[:], [[-1, W]], AluOpType.is_equal, 0.0, 0, 1).then_inc(S.pick, 1)
-    V.wait_ge(S.pick, 4)
-    V.quantize_mx(T.sq[:], T.sp[:], T.st[:]).then_inc(S.qs, 1)
+    make_pick(g, T, me)
 
-    for k in range(2):
+    def quantise_a(k):
         V.wait_ge(S["lda%d" % k], 16)
-        w = slice(2 * W * k, 2 * W * (k + 1))
-        V.quantize_mx(T.aq[:, w], T.ap[:, w], T.at[:, 2 * E * k:2 * E * (k + 1)]).then_inc(S["qa%d" % k], 1)
+        w = slice(W * CUTS[k], W * CUTS[k + 1])
+        V.quantize_mx(T.aq[:, w], T.ap[:, w], T.at[:, E * CUTS[k]:E * CUTS[k + 1]]).then_inc(S["qa%d" % k], 1)
 
     def quantise_b(k):
         tiles = loads[k]
-        w = slice(W * tiles[0], W * (tiles[-1] + 1))
         V.wait_ge(S["ldb%d" % k], 16)
+        w = slice(W * tiles[0], W * (tiles[-1] + 1))
         V.quantize_mx(T.bq[:, w], T.bp[:, w], T.bt[:, E * tiles[0]:E * (tiles[-1] + 1)]).then_inc(S["qb%d" % k], 1)
 
     def stat(i):
@@ -159,7 +204,9 @@ def rank_program(g, core, T, topo):
         k = BANK * (4 * (s % 2) + i)
         return T.ps[:, k:k + n]
 
+    quantise_a(0)
     quantise_b(0)
+    quantise_a(1)
     off = 0
     for gi, tiles in enumerate(groups):
         n = len(tiles) * W
@@ -169,8 +216,8 @@ def rank_program(g, core, T, topo):
         if gi >= 2:
             X.wait_ge(S["ev%d" % (gi - 2)], 4)
         for i in range(4):
-            if gi == 0 and i % 2 == 0:
-                X.wait_ge(S["qa%d" % (i // 2)], 1)
+            if gi == 0 and i in CUTS:
+                X.wait_ge(S["qa%d" % CUTS.index(i)], 1)
             m = X.matmul_mx(bank(gi, i, n), *stat(i), T.bq[:, w], T.bp[:, w], True, not merge)
             if not merge:
                 m.then_inc(S["mm%d_%d" % (gi, i)], 1)
@@ -181,6 +228,7 @@ def rank_program(g, core, T, topo):
             for i in range(4):
                 X.matmul_mx(bank(gi + 1, i, W), *stat(i), T.bq[:, o], T.bp[:, o], True, False)
             X.wait_ge(S.qs, 1)
+            X.wait_ge(S.sarr, got["sarr"][1])
             X.wait_ge(S.marr, got["marr"][1])
             for i in range(4):
                 X.matmul_mx(bank(gi, i, n), *pick(i), T.mq[:, 0:n], T.mp[:, 0:n], False, True).then_inc(S["mm%d_%d" % (gi, i)], 1)
@@ -201,14 +249,9 @@ def rank_program(g, core, T, topo):
             quantise_b(1)
         off += n
 
-    total, ready = 0, -1
-    for call in calls_of(T, topo, rank):
-        while ready < call[1]:
-            ready += 1
-            g.wait_ge(S["qh%d" % ready], 1)
-        total += issue(g, T, topo, core, call)
+    issue_all(g, T, topo, core, got)
 
-    order = sorted((k, name) for name, (k, _) in got.items() if name != "marr")
+    order = sorted((k, name) for name, (k, _) in got.items() if name[:3] == "arr")
     for j, (_, name) in enumerate(order):
         r = int(name[3:])
         X.wait_ge(S[name], got[name][1])
@@ -229,4 +272,3 @@ def rank_program(g, core, T, topo):
     g.sync.wait_ge(S.yev, 4)
     g.sync.dma_start(T.y[:], T.yt[:]).then_inc(S.stored, 16)
     g.sync.wait_ge(S.stored, 16)
-    g.wait_ge(S.sent, total)

from concourse.bass import DstId, RemoteDMATransfer
from concourse.mybir import dt, AluOpType, ActivationFunctionType

W = 128
E = 4 * W
BANK = 512
NR = 8
MAXG = 5
CUTS = [0, 3, 4]

SCRATCH = {
    "at": ("sbuf", [128, 4 * E], "bfloat16"),
    "bt": ("sbuf", [128, NR * E], "bfloat16"),
    "aq": ("sbuf", [128, 4 * W], "float8_e4m3fn_x4"),
    "ap": ("sbuf", [128, 4 * W], "uint8"),
    "bq": ("sbuf", [128, NR * W], "float8_e4m3fn_x4"),
    "bp": ("sbuf", [128, NR * W], "uint8"),
    "one": ("sbuf", [128, W], "bfloat16"),
    "st": ("sbuf", [128, E], "bfloat16"),
    "sq": ("sbuf", [128, 4 * W], "float8_e4m3fn_x4"),
    "sp": ("sbuf", [128, 4 * W], "uint8"),
    "ht": ("sbuf", [128, NR * E], "bfloat16"),
    "hq": ("sbuf", [128, NR * W], "float8_e4m3fn_x4"),
    "hp": ("sbuf", [128, NR * W], "uint8"),
    "rq": ("sbuf", [128, 2 * W], "float8_e4m3fn_x4"),
    "rp": ("sbuf", [128, 2 * W], "uint8"),
    "lq": ("sbuf", [128, NR * W], "float8_e4m3fn_x4"),
    "lp": ("sbuf", [128, NR * W], "uint8"),
    "mq": ("sbuf", [128, 2 * W], "float8_e4m3fn_x4"),
    "mp": ("sbuf", [128, 2 * W], "uint8"),
    "yt": ("sbuf", [128, E], "float32"),
    "ps": ("psum", [128, 8 * BANK], "float32"),
}
SEMAPHORES = (["lda0", "lda1", "fill", "pick", "qs", "qa0", "qa1", "sarr", "marr", "rqarr", "rparr", "sent", "yev", "stored"]
              + ["ldb%d" % k for k in range(5)] + ["qb%d" % k for k in range(5)]
              + ["mm%d_%d" % (k, i) for k in range(MAXG) for i in range(4)]
              + ["ev%d" % k for k in range(MAXG)] + ["qh%d" % k for k in range(MAXG)]
              + ["arr%d" % k for k in range(NR)] + ["fin%d" % i for i in range(4)])


def pairs_of(T, topo):
    hosts = {}
    for r, c in enumerate(T.cores):
        hosts.setdefault(topo.host(c), []).append(r)
    far, big = sorted(hosts.values(), key=len)
    return [big[k:k + 2] for k in range(0, len(big), 2)], far


def plan_of(T, topo, r):
    near, far = pairs_of(T, topo)
    if r in far:
        k = far.index(r)
        y = far[1 - k]
        q, m = near[2], near[1 - k]
        return y, k, [near[k], q, far, m], [near[k], q, [y], m], [(q, False), ([y], False), (m, False)]
    p = [r in q for q in near].index(True)
    k = near[p].index(r)
    y = near[p][1 - k]
    q1, q2, m = near[(p + 1) % 3], near[(p + 2) % 3], far[k]
    f = far[1 - k]
    return y, k, [[f], q1, q2, near[p], [m]], [[f], q1, q2, [y], [m]], [(q1, True), (q2, False), ([y, m], False)]


def helper_of(T, topo, r):
    c = T.cores[r]
    for d in range(256):
        if topo.host(d) == topo.host(c) and topo.chip(d) == topo.chip(c) and topo.die(d) != topo.die(c):
            return d


def share(mask, k):
    bits = [1 << e for e in range(16) if mask >> e & 1]
    n = 1
    while 2 * n * k <= len(bits):
        n *= 2
    return [sum(bits[n * j:n * j + n]) for j in range(k)]


def calls_of(T, topo, r):
    c, h = T.cores[r], helper_of(T, topo, r)
    y, k, _, groups, sends = plan_of(T, topo, r)
    flat = [t for q in groups for t in q]
    of = [gi for gi, q in enumerate(groups) for t in q]
    d = T.cores[y]
    e = topo.mask(c, d)
    near = topo.mask(c, h) & ~e
    out = []
    for part in "qp":
        out.append((c, part, ["qs"], 0, [(d, "s", W * k, "s", W * k, W, "sarr", e)]))
        out.append((h, part, ["qs"], 0, [(x, "s", W * (2 + k), "s", W * (2 + k), W, "sarr", m)
                                         for x, m in zip((c, d), share(topo.mask(h, d), 2))]))
    out += [(c, part, ["qh0"], 0, [(d, "h", 0, "m", 0, W * len(groups[0]), "marr", e)]) for part in "qp"]
    for place, (tiles, relay) in enumerate(sends):
        at = W * flat.index(tiles[0])
        waits = ["qh%d" % gi for gi in sorted({of[flat.index(t)] for t in tiles})]
        if relay:
            out += [(c, part, waits, 0, [(h, "h", at, "r", 0, W * len(tiles), "r%sarr" % part, near)]) for part in "qp"]
            ms = share(topo.mask(h, T.cores[tiles[0]]), len(tiles))
            out += [(h, part, ["r%sarr" % part], 1, [(T.cores[t], "r", W * j, "l", r * W, W, "arr%d" % r, x)
                                                     for j, (t, x) in enumerate(zip(tiles, ms))]) for part in "qp"]
        else:
            ms = share(topo.mask(c, T.cores[tiles[0]]), len(tiles))
            out += [(c, part, waits, place, [(T.cores[t], "h", W * flat.index(t), "l", r * W, W, "arr%d" % r, x)
                                             for t, x in zip(tiles, ms)]) for part in "qp"]
    return out


def issue(g, T, topo, core, call):
    part = call[1]
    items = []
    for (d, src, at, dst, to, n, sem, mask) in call[4]:
        o = T[dst + part][:, to:to + n]
        i = T[src + part][:, at:at + n]
        if part == "q":
            o, i = o.bitcast(dt.uint8), i.bitcast(dt.uint8)
        rid, pid = topo.addr(d, core)
        items.append((o, i, T.sem[sem], rid, pid, mask))
    if len(items) == 1:
        o, i, sem, rid, pid, mask = items[0]
        g.remote_dma(o, i, sem, T.sem.sent, pid, rid, mask)
    else:
        g.remote_dma_fused([RemoteDMATransfer(dst_ids=[DstId(rid=rid, pnc=pid)], dma_engine_mask=mask,
                                              remote_sem=sem, src=i, dst=o)
                            for o, i, sem, rid, pid, mask in items], local_sem=T.sem.sent)
    return sum(bin(x[5]).count("1") for x in items)


def issue_all(g, T, topo, core, got):
    total, seen = 0, []
    for r in range(NR):
        for call in calls_of(T, topo, r):
            if call[0] == core:
                for name in call[2]:
                    if name not in seen:
                        seen.append(name)
                        g.wait_ge(T.sem[name], got[name][1] if name in got else 1)
                total += issue(g, T, topo, core, call)
    g.wait_ge(T.sem.sent, total)


def arrivals(T, topo, core):
    got = {}
    for r in range(NR):
        for _, _, _, place, items in calls_of(T, topo, r):
            for x in items:
                if x[0] == core:
                    got[x[6]] = (place, got.get(x[6], (0, 0))[1] + bin(x[7]).count("1"))
    return got


def make_pick(g, T, i):
    S = T.sem
    g.vector.memset(T.one[:], 1.0).then_inc(S.fill, 1)
    g.vector.memset(T.st[:], 0.0).then_inc(S.fill, 1)
    g.wait_ge(S.fill, 2)
    g.affine_select(T.st[:, i:E:4], T.one[:], [[-1, W]], AluOpType.is_equal, 0.0, 0, 1).then_inc(S.pick, 1)
    g.vector.wait_ge(S.pick, 1)
    w = slice(W * i, W * (i + 1))
    g.vector.quantize_mx(T.sq[:, w], T.sp[:, w], T.st[:]).then_inc(S.qs, 1)


def rank_program(g, core, T, topo):
    rank = T.rank_of(core)
    got = arrivals(T, topo, core)
    if rank is None:
        helpers = [helper_of(T, topo, k) for k in range(NR)]
        if core in helpers:
            make_pick(g, T, 2 + plan_of(T, topo, helpers.index(core))[1])
            issue_all(g, T, topo, core, got)
        return
    S = T.sem
    V, X, A = g.vector, g.tensor, g.scalar
    _, me, loads, groups, _ = plan_of(T, topo, rank)
    ng = len(groups)
    where = {t: k for k, tiles in enumerate(loads) for t in tiles}

    for k in range(2):
        w = slice(E * CUTS[k], E * CUTS[k + 1])
        g.sync.dma_start(T.at[:, w], T.a[:, w]).then_inc(S["lda%d" % k], 16)
    for k, tiles in enumerate(loads):
        w = slice(E * tiles[0], E * (tiles[-1] + 1))
        (g.sync if k else g.scalar).dma_start(T.bt[:, w], T.b[:, w]).then_inc(S["ldb%d" % k], 16)

    make_pick(g, T, me)

    def quantise_a(k):
        V.wait_ge(S["lda%d" % k], 16)
        w = slice(W * CUTS[k], W * CUTS[k + 1])
        V.quantize_mx(T.aq[:, w], T.ap[:, w], T.at[:, E * CUTS[k]:E * CUTS[k + 1]]).then_inc(S["qa%d" % k], 1)

    def quantise_b(k):
        tiles = loads[k]
        V.wait_ge(S["ldb%d" % k], 16)
        w = slice(W * tiles[0], W * (tiles[-1] + 1))
        V.quantize_mx(T.bq[:, w], T.bp[:, w], T.bt[:, E * tiles[0]:E * (tiles[-1] + 1)]).then_inc(S["qb%d" % k], 1)

    def stat(i):
        return T.aq[:, W * i:W * (i + 1)], T.ap[:, W * i:W * (i + 1)]

    def pick(i):
        return T.sq[:, W * i:W * (i + 1)], T.sp[:, W * i:W * (i + 1)]

    def bank(s, i, n):
        k = BANK * (4 * (s % 2) + i)
        return T.ps[:, k:k + n]

    quantise_a(0)
    quantise_b(0)
    quantise_a(1)
    off = 0
    for gi, tiles in enumerate(groups):
        n = len(tiles) * W
        merge = gi == ng - 1
        w = slice(W * tiles[0], W * tiles[0] + n)
        X.wait_ge(S["qb%d" % where[tiles[0]]], 1)
        if gi >= 2:
            X.wait_ge(S["ev%d" % (gi - 2)], 4)
        for i in range(4):
            if gi == 0 and i in CUTS:
                X.wait_ge(S["qa%d" % CUTS.index(i)], 1)
            m = X.matmul_mx(bank(gi, i, n), *stat(i), T.bq[:, w], T.bp[:, w], True, not merge)
            if not merge:
                m.then_inc(S["mm%d_%d" % (gi, i)], 1)
        if merge:
            X.wait_ge(S["qb%d" % where[rank]], 1)
            X.wait_ge(S["ev%d" % (gi - 1)], 4)
            o = slice(W * rank, W * (rank + 1))
            for i in range(4):
                X.matmul_mx(bank(gi + 1, i, W), *stat(i), T.bq[:, o], T.bp[:, o], True, False)
            X.wait_ge(S.qs, 1)
            X.wait_ge(S.sarr, got["sarr"][1])
            X.wait_ge(S.marr, got["marr"][1])
            for i in range(4):
                X.matmul_mx(bank(gi, i, n), *pick(i), T.mq[:, 0:n], T.mp[:, 0:n], False, True).then_inc(S["mm%d_%d" % (gi, i)], 1)
        if gi > 0 and gi + 1 < len(loads):
            quantise_b(gi + 1)
        onv = (1, 3) if gi == 0 or merge else (3,)
        for i in range(4):
            out = T.ht[:, 4 * off + i:4 * (off + n):4]
            if i not in onv:
                A.wait_ge(S["mm%d_%d" % (gi, i)], 1)
                A.activation(out, bank(gi, i, n), ActivationFunctionType.Copy).then_inc(S["ev%d" % gi], 1)
            else:
                V.wait_ge(S["mm%d_%d" % (gi, i)], 1)
                V.tensor_copy(out, bank(gi, i, n)).then_inc(S["ev%d" % gi], 1)
        V.wait_ge(S["ev%d" % gi], 4)
        V.quantize_mx(T.hq[:, off:off + n], T.hp[:, off:off + n], T.ht[:, 4 * off:4 * (off + n)]).then_inc(S["qh%d" % gi], 1)
        if gi == 0:
            quantise_b(1)
        off += n

    issue_all(g, T, topo, core, got)

    order = sorted((k, name) for name, (k, _) in got.items() if name[:3] == "arr")
    for j, (_, name) in enumerate(order):
        r = int(name[3:])
        X.wait_ge(S[name], got[name][1])
        w = slice(W * r, W * (r + 1))
        end = j == len(order) - 1
        for i in range(4):
            m = X.matmul_mx(bank(ng, i, W), *pick(i), T.lq[:, w], T.lp[:, w], False, end)
            if end:
                m.then_inc(S["fin%d" % i], 1)
    for i in range(4):
        out = T.yt[:, i:E:4]
        if i % 2 == 0:
            A.wait_ge(S["fin%d" % i], 1)
            A.activation(out, bank(ng, i, W), ActivationFunctionType.Copy).then_inc(S.yev, 1)
        else:
            V.wait_ge(S["fin%d" % i], 1)
            V.tensor_copy(out, bank(ng, i, W)).then_inc(S.yev, 1)
    g.sync.wait_ge(S.yev, 4)
    g.sync.dma_start(T.y[:], T.yt[:]).then_inc(S.stored, 16)
    g.sync.wait_ge(S.stored, 16)
